import numpy as np
import ml_dtypes


def mxq(x, axis, fmt="e4m3"):
    dtype, down = {"e4m3": (ml_dtypes.float8_e4m3fn, 7), "e5m2": (ml_dtypes.float8_e5m2, 14)}[fmt]
    v = np.moveaxis(np.asarray(x, np.float32).astype(ml_dtypes.bfloat16).astype(np.float64), axis, -1)
    blocks = v.reshape(v.shape[:-1] + (-1, 32))
    amax = np.abs(blocks).max(-1, keepdims=True)
    byte = np.maximum(np.where(amax > 0, np.frexp(amax)[1] - 1 + 127, 0) - down, 1)
    scale = np.exp2(byte - 127.0)
    codes = (blocks / scale).astype(np.float32).astype(dtype).astype(np.float64)
    return np.moveaxis((codes * scale).reshape(v.shape), -1, axis)


WIDE = False


def mx_kscale(k):
    if not WIDE:
        return np.ones(k)
    levels = np.array([10, -10, 5, -5, 0])
    if k % 512:
        return np.exp2(np.random.permutation(np.resize(levels, k // 32))).repeat(32)
    a = np.empty((k // 512, 16))
    for p in range(k // 512):
        a[p, :8] = np.random.permutation(np.resize(levels, 8))
        for g in range(8):
            far = levels[np.abs(levels - a[p, g]) >= 10]
            a[p, g + 8] = far[np.random.randint(len(far))]
    return np.exp2(a.ravel()).repeat(32)


def f64(x):
    return np.asarray(x).astype(np.float64)


def striped(idx):
    return np.tile(idx.reshape(-1, 16).T, (8, 1)).astype(np.uint16)


def unstriped(offs):
    return offs[:16].T.reshape(-1).astype(np.int64)


def pack_weight(w):
    k, n = w.shape
    w = f64(np.asarray(w, np.float32).astype(ml_dtypes.bfloat16)).reshape(k // 32, 32, n)
    amax = np.abs(w).max(1)
    byte = np.clip(np.where(amax > 0, np.frexp(amax)[1] - 1 + 127 - 7, 1), 1, 254)
    scaled = (w * np.exp2(127.0 - byte)[:, None, :]).reshape(k, n).astype(np.float32)
    words = np.ascontiguousarray(scaled.reshape(k // 512, 128, 4, n).transpose(0, 1, 3, 2)).astype(ml_dtypes.float8_e4m3fn).view(np.uint8)
    return words, np.ascontiguousarray(byte.astype(np.uint8).reshape(k // 512, 16, n))


def unpack_weight(words, scales):
    g, p, n, _ = words.shape
    vals = np.ascontiguousarray(words).view(ml_dtypes.float8_e4m3fn).astype(np.float64) * np.repeat(np.exp2(scales.astype(np.float64) - 127.0), 8, axis=1)[..., None]
    return vals.transpose(0, 1, 3, 2).reshape(g * 512, n)


K, T, E, C, N = 2560, 1024, 12, 128, 128
TOP = 3
PAD = 64


def by_expert(wq, xq):
    return np.concatenate([wq[e].T @ xq[:, e * C:(e + 1) * C] for e in range(E)], axis=1)


def setup_inputs():
    n = np.random.standard_normal
    s = mx_kscale(K)[:, None]
    slot_token = np.empty(E * C, np.int64); pos = np.tile(E * C + np.arange(T) % PAD, (TOP, 1)); taken = np.zeros(T, np.int64)
    liked = np.random.randn(T)
    for e in np.random.permutation(E):
        free = np.flatnonzero(taken < TOP); pick = np.random.permutation(free[np.argsort(-(liked[free] + np.random.gumbel(size=free.size)))[:C]]); slot_token[e * C:(e + 1) * C] = pick
        pos[taken[pick], pick] = e * C + np.arange(C); taken[pick] += 1
    g = np.random.uniform(0.2, 0.8, (TOP, T))
    packed = [pack_weight(m) for m in n((E, K, N)) / np.sqrt(K) / s[None]]
    return {
        "xT": (n((K, T)) * s).astype(np.float32),
        "w_words": np.stack([m[0] for m in packed]),
        "w_scales": np.stack([m[1] for m in packed]),
        "b": (0.3 * n((N, E))).astype(np.float32),
        "gate": np.stack([np.tile(r, (N, 1)) for r in g]).astype(np.float32),
        "offs": striped(slot_token),
        "pos1": striped(pos[0]),
        "pos2": striped(pos[1]),
        "pos3": striped(pos[2]),
    }


def reference(xT, w_words, w_scales, b, gate, offs, pos1, pos2, pos3):
    idx = unstriped(offs)
    w = np.stack([unpack_weight(w_words[e], w_scales[e]) for e in range(E)])
    xq = mxq(f64(xT)[:, idx], 0, "e4m3")
    y = by_expert(w, xq)
    y = y + np.repeat(f64(b), C, axis=1)
    y = np.concatenate([y, np.zeros((N, PAD))], axis=1)
    return sum(f64(gate[r]) * y[:, unstriped(p)] for r, p in enumerate((pos1, pos2, pos3)))

@@ -1,0 +1,194 @@
+from contextlib import ExitStack
+
+import concourse.mybir as mybir
+from concourse.masks import make_identity
+
+K, T, E, C, N = 2560, 1024, 12, 128, 128
+TOP = 3
+PAD = 64
+S = E * C
+
+F32 = mybir.dt.float32
+BF16 = mybir.dt.bfloat16
+I32 = mybir.dt.int32
+U32 = mybir.dt.uint32
+U16 = mybir.dt.uint16
+U8 = mybir.dt.uint8
+FP8X4 = mybir.dt.float8_e4m3fn_x4
+COPY = mybir.ActivationFunctionType.Copy
+IDENTITY = mybir.ActivationFunctionType.Identity
+MULT = mybir.AluOpType.mult
+ADD = mybir.AluOpType.add
+
+P = 128
+PACK = 4
+K_PASS = P * PACK
+PASSES = K // K_PASS
+PER_COL = 16
+
+FLOPS = 2 * K * N * S
+BYTES = 4 * K * T + E * K * N + E * K * N // 32 + 4 * N * E + 4 * TOP * T + 2 * P * (S + TOP * T) // PER_COL + 4 * N * T
+
+FIRST_CHUNKS = (256, 256, 256, 256)
+LATER_CHUNKS = (512, 512)
+WIDE_CUTS = (0, 768, 1536)
+BYTE_CUTS = (0, 512, 1024, 1536)
+LAST_CUTS = (0, 512, 1024, 1280, 1536)
+BANK_EXPERTS = 2
+PIECE = 256
+
+
+def tile_moe_ecr_lin_bias_kernel(tc, xT, w_words, w_scales, b, gate, offs, pos1, pos2, pos3, out):
+    nc = tc.nc
+    with ExitStack() as ctx:
+        keep = ctx.enter_context(tc.tile_pool(name="keep", bufs=1))
+        ring = ctx.enter_context(tc.tile_pool(name="ring", bufs=1))
+        psum = ctx.enter_context(tc.psum_pool(name="psum", bufs=1))
+
+        def entries(tile, lo, hi):
+            return tile[:, lo // PER_COL : hi // PER_COL]
+
+        gate_cols = keep.tile([P, TOP, T // P], F32, name="gate_cols")
+        nc.scalar.dma_start(out=gate_cols[:], in_=gate[:, 0, :].rearrange("r (p c) -> p r c", p=P))
+        bias = keep.tile([P, E], F32, name="bias")
+        nc.scalar.dma_start(out=bias[:], in_=b)
+
+        first_scales = keep.tile([P, T], U8, name="first_scales", align_bytes=64)
+        later_scales = keep.tile([P, T], U8, name="later_scales", align_bytes=64)
+        w_planes = keep.tile([P, E * PASSES * N], U8, name="w_planes", align_bytes=64)
+        y = keep.tile([P, S + PAD], F32, name="y")
+        nc.vector.memset(first_scales[:].bitcast(I32), 0)
+        nc.vector.memset(w_planes[:].bitcast(I32), 0)
+        nc.vector.memset(later_scales[:].bitcast(I32), 0)
+        nc.vector.memset(y[:, S:], 0.0)
+        ident = keep.tile([P, P], F32, name="ident")
+        make_identity(nc, ident[:])
+
+        raw = {}
+        slots = keep.tile([P, S // PER_COL], U16, name="slots")
+        for a in range(PASSES):
+            rows = xT[a * K_PASS : (a + 1) * K_PASS, :].rearrange("(p j) t -> p j t", j=PACK)
+            t0 = 0
+            for width in FIRST_CHUNKS if a == 0 else LATER_CHUNKS:
+                raw[a, t0] = keep.tile([P, PACK, width], F32, name=f"raw{a}_{t0}")
+                nc.sync.dma_start(out=raw[a, t0][:], in_=rows[:, :, t0 : t0 + width])
+                t0 += width
+            if a == 0:
+                nc.sync.dma_start(slots[:], offs)
+        places = []
+        for r, pos in enumerate((pos1, pos2, pos3)):
+            place = keep.tile([P, T // PER_COL], U16, name=f"place{r}")
+            nc.sync.dma_start(place[:], pos)
+            places.append(place)
+        scale_rows = w_scales.rearrange("e a (q i) n -> i q (e a) n", i=4)
+        for i in range(4):
+            nc.sync.dma_start(
+                out=w_planes[i:P:32, :].rearrange("q (m n) -> q m n", n=N).bitcast(I32),
+                in_=scale_rows[i].bitcast(I32),
+            )
+        weights = {}
+        for a in range(PASSES):
+            group = E if a < PASSES - 1 else 4
+            for e0 in range(0, E, group):
+                w_tile = keep.tile([P, group, N * PACK], U8, name=f"w{a}_{e0}", align_bytes=64)
+                nc.sync.dma_start(
+                    out=w_tile[:].bitcast(I32),
+                    in_=w_words[e0 : e0 + group, a].rearrange("e p n j -> p e (n j)").bitcast(I32),
+                )
+                for e in range(e0, e0 + group):
+                    weights[a, e] = w_tile[:, e - e0, :]
+
+        gates = keep.tile([P, TOP, T], F32, name="gates")
+        per_part = T // P
+        for r in range(TOP):
+            for c0 in range(0, per_part, 4):
+                spread = psum.tile([P, 4, P], F32, name="spread", bufs=2)
+                for c in range(4):
+                    nc.tensor.transpose(
+                        spread[:, c, :], gate_cols[:, r, c0 + c : c0 + c + 1].to_broadcast([P, P]), ident[:]
+                    )
+                nc.scalar.activation(
+                    gates[:, r, :].rearrange("n (p c) -> n p c", c=per_part)[:, :, c0 : c0 + 4],
+                    spread[:].rearrange("n c p -> n p c"),
+                    COPY,
+                )
+
+        first_slot_scales = keep.tile([P, S], U8, name="first_slot_scales", align_bytes=64)
+        later_slot_scales = keep.tile([P, S], U8, name="later_slot_scales", align_bytes=64)
+        slot_codes = []
+        for a in range(PASSES):
+            codes = ring.tile([P, T], U32, name="codes", bufs=3, align_bytes=64)
+            t0 = 0
+            for width in FIRST_CHUNKS if a == 0 else LATER_CHUNKS:
+                grouped = ring.tile([P, width * PACK], BF16, name="grouped", bufs=4, align_bytes=64)
+                dst = grouped[:].rearrange("p (c i j) -> p c j i", i=4, j=PACK)
+                src = raw[a, t0][:].rearrange("p j (c i) -> p c j i", i=4)
+                if a == 0:
+                    nc.vector.tensor_copy(out=dst, in_=src)
+                    plane = first_scales[:, t0 : t0 + width]
+                else:
+                    nc.scalar.activation(dst, src, COPY)
+                    plane = later_scales[4 * (a - 1) :, t0 : t0 + width]
+                nc.vector.quantize_mx(out=codes[:, t0 : t0 + width].bitcast(FP8X4), scales=plane, in_=grouped[:])
+                t0 += width
+            gathered = keep.tile([P, S], U32, name=f"slot_codes{a}", align_bytes=64)
+            slot_codes.append(gathered)
+            if a == PASSES - 1:
+                for lo, hi in zip(BYTE_CUTS, BYTE_CUTS[1:]):
+                    nc.vector.tensor_copy(later_slot_scales[:, lo:hi], later_scales[:].indirect(entries(slots, lo, hi)))
+            cuts = WIDE_CUTS if a < PASSES - 1 else LAST_CUTS
+            for lo, hi in zip(cuts, cuts[1:]):
+                nc.vector.tensor_copy(gathered[:, lo:hi], codes[:].indirect(entries(slots, lo, hi)))
+            if a == 0:
+                for lo, hi in zip(WIDE_CUTS, WIDE_CUTS[1:]):
+                    nc.vector.tensor_copy(first_slot_scales[:, lo:hi], first_scales[:].indirect(entries(slots, lo, hi)))
+
+        banks = [psum.tile([P, BANK_EXPERTS * C], F32, name=f"bank{g}") for g in range(E // BANK_EXPERTS)]
+        for a in range(PASSES):
+            for e in range(E):
+                g, m = divmod(e, BANK_EXPERTS)
+                cols = slice(e * C, (e + 1) * C)
+                plane = first_slot_scales[:, cols] if a == 0 else later_slot_scales[4 * (a - 1) :, cols]
+                block = e * PASSES + a
+                nc.tensor.matmul_mx(
+                    out=banks[g][:, m * C : (m + 1) * C],
+                    lhsT=weights[a, e].bitcast(FP8X4),
+                    lhsT_scale=w_planes[:, block * N : (block + 1) * N],
+                    rhs=slot_codes[a][:, cols].bitcast(FP8X4),
+                    rhs_scale=plane,
+                    start=(a == 0 and m == 0),
+                    stop=(a == PASSES - 1 and m == BANK_EXPERTS - 1),
+                )
+        for g, bank in enumerate(banks):
+            e0 = g * BANK_EXPERTS
+            if g < len(banks) - 1:
+                for m in range(BANK_EXPERTS):
+                    e = e0 + m
+                    nc.scalar.activation(
+                        y[:, e * C : (e + 1) * C], bank[:, m * C : (m + 1) * C], IDENTITY, bias=bias[:, e : e + 1]
+                    )
+            else:
+                nc.vector.tensor_tensor(
+                    y[:, e0 * C : (e0 + BANK_EXPERTS) * C].rearrange("n (m c) -> n m c", c=C),
+                    bank[:].rearrange("n (m c) -> n m c", c=C),
+                    bias[:, e0 : e0 + BANK_EXPERTS].unsqueeze(2).to_broadcast([P, BANK_EXPERTS, C]),
+                    ADD,
+                )
+
+        first = keep.tile([P, T], F32, name="first")
+        for lo in range(0, T, 512):
+            nc.vector.tensor_tensor(
+                first[:, lo : lo + 512], y[:].indirect(entries(places[0], lo, lo + 512)), gates[:, 0, lo : lo + 512], MULT
+            )
+        for lo in range(0, T, PIECE):
+            hi = lo + PIECE
+            fetched = ring.tile([P, TOP - 1, PIECE], F32, name="fetched", bufs=T // PIECE)
+            for r in range(1, TOP):
+                nc.scalar.activation(fetched[:, r - 1, :], y[:].indirect(entries(places[r], lo, hi)), COPY)
+            weighed = ring.tile([P, TOP - 1, PIECE], F32, name="weighed", bufs=2)
+            nc.vector.tensor_tensor(weighed[:], fetched[:], gates[:, 1:TOP, lo:hi], MULT)
+            partial = ring.tile([P, PIECE], F32, name="partial", bufs=2)
+            nc.vector.tensor_tensor(partial[:], weighed[:, 0, :], first[:, lo:hi], ADD)
+            result = ring.tile([P, PIECE], F32, name="result", bufs=T // PIECE)
+            nc.vector.tensor_tensor(result[:], partial[:], weighed[:, 1, :], ADD)
+            nc.sync.dma_start(out=out[:, lo:hi], in_=result[:])

@@ -29,13 +29,13 @@ PER_COL = 16
 FLOPS = 2 * K * N * S
 BYTES = 4 * K * T + E * K * N + E * K * N // 32 + 4 * N * E + 4 * TOP * T + 2 * P * (S + TOP * T) // PER_COL + 4 * N * T
 
-FIRST_CHUNKS = (256, 256, 256, 256)
-LATER_CHUNKS = (512, 512)
+CHUNKS = ((256, 256, 256, 128, 128), (256, 256, 512), (512, 512), (512, 512), (512, 512))
 WIDE_CUTS = (0, 768, 1536)
-BYTE_CUTS = (0, 512, 1024, 1536)
 LAST_CUTS = (0, 512, 1024, 1280, 1536)
-BANK_EXPERTS = 2
-PIECE = 256
+WEIGHT_CUTS = (0, 4, 8, 10, 11, 12)
+BANK_CUTS = (0, 2, 4, 6, 8, 10, 11, 12)
+PIECE_CUTS = (0, 256, 512, 768, 1024)
+FUSED_CUTS = (0, 512, 1024)
 
 
 def tile_moe_ecr_lin_bias_kernel(tc, xT, w_words, w_scales, b, gate, offs, pos1, pos2, pos3, out):
@@ -49,32 +49,34 @@ def tile_moe_ecr_lin_bias_kernel(tc, xT, w_words, w_scales, b, gate, offs, pos1,
             return tile[:, lo // PER_COL : hi // PER_COL]
 
         gate_cols = keep.tile([P, TOP, T // P], F32, name="gate_cols")
-        nc.scalar.dma_start(out=gate_cols[:], in_=gate[:, 0, :].rearrange("r (p c) -> p r c", p=P))
         bias = keep.tile([P, E], F32, name="bias")
-        nc.scalar.dma_start(out=bias[:], in_=b)
 
         first_scales = keep.tile([P, T], U8, name="first_scales", align_bytes=64)
         later_scales = keep.tile([P, T], U8, name="later_scales", align_bytes=64)
         w_planes = keep.tile([P, E * PASSES * N], U8, name="w_planes", align_bytes=64)
         y = keep.tile([P, S + PAD], F32, name="y")
-        nc.vector.memset(first_scales[:].bitcast(I32), 0)
-        nc.vector.memset(w_planes[:].bitcast(I32), 0)
-        nc.vector.memset(later_scales[:].bitcast(I32), 0)
-        nc.vector.memset(y[:, S:], 0.0)
         ident = keep.tile([P, P], F32, name="ident")
         make_identity(nc, ident[:])
+        nc.vector.memset(w_planes[:].bitcast(I32), 0)
+        nc.gpsimd.memset(first_scales[:].bitcast(I32), 0)
+        nc.gpsimd.memset(later_scales[:].bitcast(I32), 0)
+        nc.gpsimd.memset(y[:, S:], 0.0)
 
         raw = {}
         slots = keep.tile([P, S // PER_COL], U16, name="slots")
         for a in range(PASSES):
             rows = xT[a * K_PASS : (a + 1) * K_PASS, :].rearrange("(p j) t -> p j t", j=PACK)
             t0 = 0
-            for width in FIRST_CHUNKS if a == 0 else LATER_CHUNKS:
-                raw[a, t0] = keep.tile([P, PACK, width], F32, name=f"raw{a}_{t0}")
+            for width in CHUNKS[a]:
+                last_load = a == PASSES - 1 and t0 + width == T
+                raw[a, t0] = keep.tile([P, PACK, width], F32, name="raw", tag="handover" if last_load else f"raw{a}_{t0}")
                 nc.sync.dma_start(out=raw[a, t0][:], in_=rows[:, :, t0 : t0 + width])
                 t0 += width
             if a == 0:
                 nc.sync.dma_start(slots[:], offs)
+            if a == 1:
+                nc.sync.dma_start(out=gate_cols[:], in_=gate[:, 0, :].rearrange("r (p c) -> p r c", p=P))
+                nc.sync.dma_start(out=bias[:], in_=b)
         places = []
         for r, pos in enumerate((pos1, pos2, pos3)):
             place = keep.tile([P, T // PER_COL], U16, name=f"place{r}")
@@ -86,23 +88,53 @@ def tile_moe_ecr_lin_bias_kernel(tc, xT, w_words, w_scales, b, gate, offs, pos1,
                 out=w_planes[i:P:32, :].rearrange("q (m n) -> q m n", n=N).bitcast(I32),
                 in_=scale_rows[i].bitcast(I32),
             )
-        weights = {}
-        for a in range(PASSES):
-            group = E if a < PASSES - 1 else 4
-            for e0 in range(0, E, group):
-                w_tile = keep.tile([P, group, N * PACK], U8, name=f"w{a}_{e0}", align_bytes=64)
-                nc.sync.dma_start(
-                    out=w_tile[:].bitcast(I32),
-                    in_=w_words[e0 : e0 + group, a].rearrange("e p n j -> p e (n j)").bitcast(I32),
-                )
-                for e in range(e0, e0 + group):
-                    weights[a, e] = w_tile[:, e - e0, :]
 
-        gates = keep.tile([P, TOP, T], F32, name="gates")
+        weights = {}
+        for e0, e1 in zip(WEIGHT_CUTS, WEIGHT_CUTS[1:]):
+            w_tile = keep.tile([P, (e1 - e0) * PASSES, N * PACK], U8, name=f"w{e0}", align_bytes=64)
+            nc.sync.dma_start(
+                out=w_tile[:].bitcast(I32),
+                in_=w_words[e0:e1].rearrange("e a p n j -> p (e a) (n j)").bitcast(I32),
+            )
+            for e in range(e0, e1):
+                for a in range(PASSES):
+                    weights[a, e] = w_tile[:, (e - e0) * PASSES + a, :]
+
+        first_slot_scales = keep.tile([P, S], U8, name="first_slot_scales", align_bytes=64)
+        later_slot_scales = keep.tile([P, S], U8, name="later_slot_scales", align_bytes=64)
+        slot_codes = []
+        for a in range(PASSES):
+            codes = ring.tile([P, T], U32, name="codes", bufs=3, align_bytes=64)
+            t0 = 0
+            for width in CHUNKS[a]:
+                grouped = ring.tile([P, width * PACK], BF16, name="grouped", bufs=4, align_bytes=64)
+                dst = grouped[:].rearrange("p (c i j) -> p c j i", i=4, j=PACK)
+                src = raw[a, t0][:].rearrange("p j (c i) -> p c j i", i=4)
+                if a == 0 and t0 > 0:
+                    nc.vector.tensor_copy(out=dst, in_=src)
+                else:
+                    nc.scalar.activation(dst, src, COPY)
+                plane = first_scales[:, t0 : t0 + width] if a == 0 else later_scales[4 * (a - 1) :, t0 : t0 + width]
+                nc.vector.quantize_mx(out=codes[:, t0 : t0 + width].bitcast(FP8X4), scales=plane, in_=grouped[:])
+                t0 += width
+            gathered = keep.tile([P, S], U32, name=f"slot_codes{a}", align_bytes=64)
+            slot_codes.append(gathered)
+            cuts = WIDE_CUTS if a < PASSES - 1 else LAST_CUTS
+            for lo, hi in zip(cuts, cuts[1:]):
+                if a == PASSES - 1:
+                    nc.vector.tensor_copy(later_slot_scales[:, lo:hi], later_scales[:].indirect(entries(slots, lo, hi)))
+                step = C if (a, hi) == (PASSES - 1, S) else hi - lo
+                for w0 in range(lo, hi, step):
+                    nc.vector.tensor_copy(gathered[:, w0 : w0 + step], codes[:].indirect(entries(slots, w0, w0 + step)))
+            if a == 0:
+                for lo, hi in zip(WIDE_CUTS, WIDE_CUTS[1:]):
+                    nc.vector.tensor_copy(first_slot_scales[:, lo:hi], first_scales[:].indirect(entries(slots, lo, hi)))
+
+        gates = keep.tile([P, TOP, T], F32, name="gates", tag="handover")
         per_part = T // P
         for r in range(TOP):
             for c0 in range(0, per_part, 4):
-                spread = psum.tile([P, 4, P], F32, name="spread", bufs=2)
+                spread = psum.tile([P, 4, P], F32, name="spread", tag=f"bank{2 * r + c0 // 4}")
                 for c in range(4):
                     nc.tensor.transpose(
                         spread[:, c, :], gate_cols[:, r, c0 + c : c0 + c + 1].to_broadcast([P, P]), ident[:]
@@ -113,82 +145,40 @@ def tile_moe_ecr_lin_bias_kernel(tc, xT, w_words, w_scales, b, gate, offs, pos1,
                     COPY,
                 )
 
-        first_slot_scales = keep.tile([P, S], U8, name="first_slot_scales", align_bytes=64)
-        later_slot_scales = keep.tile([P, S], U8, name="later_slot_scales", align_bytes=64)
-        slot_codes = []
-        for a in range(PASSES):
-            codes = ring.tile([P, T], U32, name="codes", bufs=3, align_bytes=64)
-            t0 = 0
-            for width in FIRST_CHUNKS if a == 0 else LATER_CHUNKS:
-                grouped = ring.tile([P, width * PACK], BF16, name="grouped", bufs=4, align_bytes=64)
-                dst = grouped[:].rearrange("p (c i j) -> p c j i", i=4, j=PACK)
-                src = raw[a, t0][:].rearrange("p j (c i) -> p c j i", i=4)
-                if a == 0:
-                    nc.vector.tensor_copy(out=dst, in_=src)
-                    plane = first_scales[:, t0 : t0 + width]
-                else:
-                    nc.scalar.activation(dst, src, COPY)
-                    plane = later_scales[4 * (a - 1) :, t0 : t0 + width]
-                nc.vector.quantize_mx(out=codes[:, t0 : t0 + width].bitcast(FP8X4), scales=plane, in_=grouped[:])
-                t0 += width
-            gathered = keep.tile([P, S], U32, name=f"slot_codes{a}", align_bytes=64)
-            slot_codes.append(gathered)
-            if a == PASSES - 1:
-                for lo, hi in zip(BYTE_CUTS, BYTE_CUTS[1:]):
-                    nc.vector.tensor_copy(later_slot_scales[:, lo:hi], later_scales[:].indirect(entries(slots, lo, hi)))
-            cuts = WIDE_CUTS if a < PASSES - 1 else LAST_CUTS
-            for lo, hi in zip(cuts, cuts[1:]):
-                nc.vector.tensor_copy(gathered[:, lo:hi], codes[:].indirect(entries(slots, lo, hi)))
-            if a == 0:
-                for lo, hi in zip(WIDE_CUTS, WIDE_CUTS[1:]):
-                    nc.vector.tensor_copy(first_slot_scales[:, lo:hi], first_scales[:].indirect(entries(slots, lo, hi)))
-
-        banks = [psum.tile([P, BANK_EXPERTS * C], F32, name=f"bank{g}") for g in range(E // BANK_EXPERTS)]
-        for a in range(PASSES):
-            for e in range(E):
-                g, m = divmod(e, BANK_EXPERTS)
-                cols = slice(e * C, (e + 1) * C)
-                plane = first_slot_scales[:, cols] if a == 0 else later_slot_scales[4 * (a - 1) :, cols]
-                block = e * PASSES + a
-                nc.tensor.matmul_mx(
-                    out=banks[g][:, m * C : (m + 1) * C],
-                    lhsT=weights[a, e].bitcast(FP8X4),
-                    lhsT_scale=w_planes[:, block * N : (block + 1) * N],
-                    rhs=slot_codes[a][:, cols].bitcast(FP8X4),
-                    rhs_scale=plane,
-                    start=(a == 0 and m == 0),
-                    stop=(a == PASSES - 1 and m == BANK_EXPERTS - 1),
-                )
-        for g, bank in enumerate(banks):
-            e0 = g * BANK_EXPERTS
-            if g < len(banks) - 1:
-                for m in range(BANK_EXPERTS):
-                    e = e0 + m
-                    nc.scalar.activation(
-                        y[:, e * C : (e + 1) * C], bank[:, m * C : (m + 1) * C], IDENTITY, bias=bias[:, e : e + 1]
+        for g, (e0, e1) in enumerate(zip(BANK_CUTS, BANK_CUTS[1:])):
+            bank = psum.tile([P, (e1 - e0) * C], F32, name="bank", tag=f"bank{g}")
+            for a in range(PASSES):
+                for e in range(e0, e1):
+                    cols = slice(e * C, (e + 1) * C)
+                    plane = first_slot_scales[:, cols] if a == 0 else later_slot_scales[4 * (a - 1) :, cols]
+                    block = e * PASSES + a
+                    nc.tensor.matmul_mx(
+                        out=bank[:, (e - e0) * C : (e - e0 + 1) * C],
+                        lhsT=weights[a, e].bitcast(FP8X4),
+                        lhsT_scale=w_planes[:, block * N : (block + 1) * N],
+                        rhs=slot_codes[a][:, cols].bitcast(FP8X4),
+                        rhs_scale=plane,
+                        start=(a == 0 and e == e0),
+                        stop=(a == PASSES - 1 and e == e1 - 1),
                     )
-            else:
-                nc.vector.tensor_tensor(
-                    y[:, e0 * C : (e0 + BANK_EXPERTS) * C].rearrange("n (m c) -> n m c", c=C),
-                    bank[:].rearrange("n (m c) -> n m c", c=C),
-                    bias[:, e0 : e0 + BANK_EXPERTS].unsqueeze(2).to_broadcast([P, BANK_EXPERTS, C]),
-                    ADD,
-                )
+            for e in range(e0, e1):
+                sums = bank[:, (e - e0) * C : (e - e0 + 1) * C]
+                if e < E - 1:
+                    nc.scalar.activation(y[:, e * C : (e + 1) * C], sums, IDENTITY, bias=bias[:, e : e + 1])
+                else:
+                    nc.vector.tensor_scalar_add(y[:, e * C : (e + 1) * C], sums, bias[:, e : e + 1])
 
-        first = keep.tile([P, T], F32, name="first")
-        for lo in range(0, T, 512):
-            nc.vector.tensor_tensor(
-                first[:, lo : lo + 512], y[:].indirect(entries(places[0], lo, lo + 512)), gates[:, 0, lo : lo + 512], MULT
-            )
-        for lo in range(0, T, PIECE):
-            hi = lo + PIECE
-            fetched = ring.tile([P, TOP - 1, PIECE], F32, name="fetched", bufs=T // PIECE)
+        fused = keep.tile([P, T], F32, name="fused")
+        for lo, hi in zip(FUSED_CUTS, FUSED_CUTS[1:]):
+            nc.vector.tensor_tensor(fused[:, lo:hi], y[:].indirect(entries(places[0], lo, hi)), gates[:, 0, lo:hi], MULT)
+        for lo, hi in zip(PIECE_CUTS, PIECE_CUTS[1:]):
+            fetched = keep.tile([P, TOP - 1, hi - lo], F32, name=f"fetched{lo}")
             for r in range(1, TOP):
                 nc.scalar.activation(fetched[:, r - 1, :], y[:].indirect(entries(places[r], lo, hi)), COPY)
-            weighed = ring.tile([P, TOP - 1, PIECE], F32, name="weighed", bufs=2)
+            weighed = keep.tile([P, TOP - 1, hi - lo], F32, name=f"weighed{lo}")
             nc.vector.tensor_tensor(weighed[:], fetched[:], gates[:, 1:TOP, lo:hi], MULT)
-            partial = ring.tile([P, PIECE], F32, name="partial", bufs=2)
-            nc.vector.tensor_tensor(partial[:], weighed[:, 0, :], first[:, lo:hi], ADD)
-            result = ring.tile([P, PIECE], F32, name="result", bufs=T // PIECE)
+            partial = keep.tile([P, hi - lo], F32, name=f"partial{lo}")
+            nc.vector.tensor_tensor(partial[:], weighed[:, 0, :], fused[:, lo:hi], ADD)
+            result = keep.tile([P, hi - lo], F32, name=f"result{lo}")
             nc.vector.tensor_tensor(result[:], partial[:], weighed[:, 1, :], ADD)
             nc.sync.dma_start(out=out[:, lo:hi], in_=result[:])

from contextlib import ExitStack

import concourse.mybir as mybir
from concourse.masks import make_identity

K, T, E, C, N = 2560, 1024, 12, 128, 128
TOP = 3
PAD = 64
S = E * C

F32 = mybir.dt.float32
BF16 = mybir.dt.bfloat16
I32 = mybir.dt.int32
U32 = mybir.dt.uint32
U16 = mybir.dt.uint16
U8 = mybir.dt.uint8
FP8X4 = mybir.dt.float8_e4m3fn_x4
COPY = mybir.ActivationFunctionType.Copy
IDENTITY = mybir.ActivationFunctionType.Identity
MULT = mybir.AluOpType.mult
ADD = mybir.AluOpType.add

P = 128
PACK = 4
K_PASS = P * PACK
PASSES = K // K_PASS
PER_COL = 16

FLOPS = 2 * K * N * S
BYTES = 4 * K * T + E * K * N + E * K * N // 32 + 4 * N * E + 4 * TOP * T + 2 * P * (S + TOP * T) // PER_COL + 4 * N * T

CHUNKS = ((256, 256, 256, 128, 128), (256, 256, 512), (512, 512), (512, 512), (512, 512))
WIDE_CUTS = (0, 768, 1536)
LAST_CUTS = (0, 512, 1024, 1280, 1536)
WEIGHT_CUTS = (0, 4, 8, 10, 11, 12)
BANK_CUTS = (0, 2, 4, 6, 8, 10, 11, 12)
PIECE_CUTS = (0, 256, 512, 768, 1024)
FUSED_CUTS = (0, 512, 1024)


def tile_moe_ecr_lin_bias_kernel(tc, xT, w_words, w_scales, b, gate, offs, pos1, pos2, pos3, out):
    nc = tc.nc
    with ExitStack() as ctx:
        keep = ctx.enter_context(tc.tile_pool(name="keep", bufs=1))
        ring = ctx.enter_context(tc.tile_pool(name="ring", bufs=1))
        psum = ctx.enter_context(tc.psum_pool(name="psum", bufs=1))

        def entries(tile, lo, hi):
            return tile[:, lo // PER_COL : hi // PER_COL]

        gate_cols = keep.tile([P, TOP, T // P], F32, name="gate_cols")
        bias = keep.tile([P, E], F32, name="bias")

        first_scales = keep.tile([P, T], U8, name="first_scales", align_bytes=64)
        later_scales = keep.tile([P, T], U8, name="later_scales", align_bytes=64)
        w_planes = keep.tile([P, E * PASSES * N], U8, name="w_planes", align_bytes=64)
        y = keep.tile([P, S + PAD], F32, name="y")
        ident = keep.tile([P, P], F32, name="ident")
        make_identity(nc, ident[:])
        nc.vector.memset(w_planes[:].bitcast(I32), 0)
        nc.gpsimd.memset(first_scales[:].bitcast(I32), 0)
        nc.gpsimd.memset(later_scales[:].bitcast(I32), 0)
        nc.gpsimd.memset(y[:, S:], 0.0)

        raw = {}
        slots = keep.tile([P, S // PER_COL], U16, name="slots")
        for a in range(PASSES):
            rows = xT[a * K_PASS : (a + 1) * K_PASS, :].rearrange("(p j) t -> p j t", j=PACK)
            t0 = 0
            for width in CHUNKS[a]:
                last_load = a == PASSES - 1 and t0 + width == T
                raw[a, t0] = keep.tile([P, PACK, width], F32, name="raw", tag="handover" if last_load else f"raw{a}_{t0}")
                nc.sync.dma_start(out=raw[a, t0][:], in_=rows[:, :, t0 : t0 + width])
                t0 += width
            if a == 0:
                nc.sync.dma_start(slots[:], offs)
            if a == 1:
                nc.sync.dma_start(out=gate_cols[:], in_=gate[:, 0, :].rearrange("r (p c) -> p r c", p=P))
                nc.sync.dma_start(out=bias[:], in_=b)
        places = []
        for r, pos in enumerate((pos1, pos2, pos3)):
            place = keep.tile([P, T // PER_COL], U16, name=f"place{r}")
            nc.sync.dma_start(place[:], pos)
            places.append(place)
        scale_rows = w_scales.rearrange("e a (q i) n -> i q (e a) n", i=4)
        for i in range(4):
            nc.sync.dma_start(
                out=w_planes[i:P:32, :].rearrange("q (m n) -> q m n", n=N).bitcast(I32),
                in_=scale_rows[i].bitcast(I32),
            )

        weights = {}
        for e0, e1 in zip(WEIGHT_CUTS, WEIGHT_CUTS[1:]):
            w_tile = keep.tile([P, (e1 - e0) * PASSES, N * PACK], U8, name=f"w{e0}", align_bytes=64)
            nc.sync.dma_start(
                out=w_tile[:].bitcast(I32),
                in_=w_words[e0:e1].rearrange("e a p n j -> p (e a) (n j)").bitcast(I32),
            )
            for e in range(e0, e1):
                for a in range(PASSES):
                    weights[a, e] = w_tile[:, (e - e0) * PASSES + a, :]

        first_slot_scales = keep.tile([P, S], U8, name="first_slot_scales", align_bytes=64)
        later_slot_scales = keep.tile([P, S], U8, name="later_slot_scales", align_bytes=64)
        slot_codes = []
        for a in range(PASSES):
            codes = ring.tile([P, T], U32, name="codes", bufs=3, align_bytes=64)
            t0 = 0
            for width in CHUNKS[a]:
                grouped = ring.tile([P, width * PACK], BF16, name="grouped", bufs=4, align_bytes=64)
                dst = grouped[:].rearrange("p (c i j) -> p c j i", i=4, j=PACK)
                src = raw[a, t0][:].rearrange("p j (c i) -> p c j i", i=4)
                if a == 0 and t0 > 0:
                    nc.vector.tensor_copy(out=dst, in_=src)
                else:
                    nc.scalar.activation(dst, src, COPY)
                plane = first_scales[:, t0 : t0 + width] if a == 0 else later_scales[4 * (a - 1) :, t0 : t0 + width]
                nc.vector.quantize_mx(out=codes[:, t0 : t0 + width].bitcast(FP8X4), scales=plane, in_=grouped[:])
                t0 += width
            gathered = keep.tile([P, S], U32, name=f"slot_codes{a}", align_bytes=64)
            slot_codes.append(gathered)
            cuts = WIDE_CUTS if a < PASSES - 1 else LAST_CUTS
            for lo, hi in zip(cuts, cuts[1:]):
                if a == PASSES - 1:
                    nc.vector.tensor_copy(later_slot_scales[:, lo:hi], later_scales[:].indirect(entries(slots, lo, hi)))
                step = C if (a, hi) == (PASSES - 1, S) else hi - lo
                for w0 in range(lo, hi, step):
                    nc.vector.tensor_copy(gathered[:, w0 : w0 + step], codes[:].indirect(entries(slots, w0, w0 + step)))
            if a == 0:
                for lo, hi in zip(WIDE_CUTS, WIDE_CUTS[1:]):
                    nc.vector.tensor_copy(first_slot_scales[:, lo:hi], first_scales[:].indirect(entries(slots, lo, hi)))

        gates = keep.tile([P, TOP, T], F32, name="gates", tag="handover")
        per_part = T // P
        for r in range(TOP):
            for c0 in range(0, per_part, 4):
                spread = psum.tile([P, 4, P], F32, name="spread", tag=f"bank{2 * r + c0 // 4}")
                for c in range(4):
                    nc.tensor.transpose(
                        spread[:, c, :], gate_cols[:, r, c0 + c : c0 + c + 1].to_broadcast([P, P]), ident[:]
                    )
                nc.scalar.activation(
                    gates[:, r, :].rearrange("n (p c) -> n p c", c=per_part)[:, :, c0 : c0 + 4],
                    spread[:].rearrange("n c p -> n p c"),
                    COPY,
                )

        for g, (e0, e1) in enumerate(zip(BANK_CUTS, BANK_CUTS[1:])):
            bank = psum.tile([P, (e1 - e0) * C], F32, name="bank", tag=f"bank{g}")
            for a in range(PASSES):
                for e in range(e0, e1):
                    cols = slice(e * C, (e + 1) * C)
                    plane = first_slot_scales[:, cols] if a == 0 else later_slot_scales[4 * (a - 1) :, cols]
                    block = e * PASSES + a
                    nc.tensor.matmul_mx(
                        out=bank[:, (e - e0) * C : (e - e0 + 1) * C],
                        lhsT=weights[a, e].bitcast(FP8X4),
                        lhsT_scale=w_planes[:, block * N : (block + 1) * N],
                        rhs=slot_codes[a][:, cols].bitcast(FP8X4),
                        rhs_scale=plane,
                        start=(a == 0 and e == e0),
                        stop=(a == PASSES - 1 and e == e1 - 1),
                    )
            for e in range(e0, e1):
                sums = bank[:, (e - e0) * C : (e - e0 + 1) * C]
                if e < E - 1:
                    nc.scalar.activation(y[:, e * C : (e + 1) * C], sums, IDENTITY, bias=bias[:, e : e + 1])
                else:
                    nc.vector.tensor_scalar_add(y[:, e * C : (e + 1) * C], sums, bias[:, e : e + 1])

        fused = keep.tile([P, T], F32, name="fused")
        for lo, hi in zip(FUSED_CUTS, FUSED_CUTS[1:]):
            nc.vector.tensor_tensor(fused[:, lo:hi], y[:].indirect(entries(places[0], lo, hi)), gates[:, 0, lo:hi], MULT)
        for lo, hi in zip(PIECE_CUTS, PIECE_CUTS[1:]):
            fetched = keep.tile([P, TOP - 1, hi - lo], F32, name=f"fetched{lo}")
            for r in range(1, TOP):
                nc.scalar.activation(fetched[:, r - 1, :], y[:].indirect(entries(places[r], lo, hi)), COPY)
            weighed = keep.tile([P, TOP - 1, hi - lo], F32, name=f"weighed{lo}")
            nc.vector.tensor_tensor(weighed[:], fetched[:], gates[:, 1:TOP, lo:hi], MULT)
            partial = keep.tile([P, hi - lo], F32, name=f"partial{lo}")
            nc.vector.tensor_tensor(partial[:], weighed[:, 0, :], fused[:, lo:hi], ADD)
            result = keep.tile([P, hi - lo], F32, name=f"result{lo}")
            nc.vector.tensor_tensor(result[:], partial[:], weighed[:, 1, :], ADD)
            nc.sync.dma_start(out=out[:, lo:hi], in_=result[:])
